import numpy as np
import ml_dtypes


def mxq(x, axis, fmt="e4m3"):
    dtype, down = {"e4m3": (ml_dtypes.float8_e4m3fn, 7), "e5m2": (ml_dtypes.float8_e5m2, 14)}[fmt]
    v = np.moveaxis(np.asarray(x, np.float32).astype(ml_dtypes.bfloat16).astype(np.float64), axis, -1)
    blocks = v.reshape(v.shape[:-1] + (-1, 32))
    amax = np.abs(blocks).max(-1, keepdims=True)
    byte = np.maximum(np.where(amax > 0, np.frexp(amax)[1] - 1 + 127, 0) - down, 1)
    scale = np.exp2(byte - 127.0)
    codes = (blocks / scale).astype(np.float32).astype(dtype).astype(np.float64)
    return np.moveaxis((codes * scale).reshape(v.shape), -1, axis)


WIDE = False


def mx_kscale(k):
    if not WIDE:
        return np.ones(k)
    levels = np.array([10, -10, 5, -5, 0])
    if k % 512:
        return np.exp2(np.random.permutation(np.resize(levels, k // 32))).repeat(32)
    a = np.empty((k // 512, 16))
    for p in range(k // 512):
        a[p, :8] = np.random.permutation(np.resize(levels, 8))
        for g in range(8):
            far = levels[np.abs(levels - a[p, g]) >= 10]
            a[p, g + 8] = far[np.random.randint(len(far))]
    return np.exp2(a.ravel()).repeat(32)


def f64(x):
    return np.asarray(x).astype(np.float64)


def striped(idx):
    return np.tile(idx.reshape(-1, 16).T, (8, 1)).astype(np.uint16)


def unstriped(offs):
    return offs[:16].T.reshape(-1).astype(np.int64)


def gelu(v):
    return 0.5 * v * (1.0 + np.tanh(np.sqrt(2.0 / np.pi) * (v + 0.044715 * v**3)))


K, T, E, C, N = 2048, 1024, 16, 128, 128


def by_expert(wq, xq):
    return np.concatenate([wq[e].T @ xq[:, e * C:(e + 1) * C] for e in range(E)], axis=1)


def setup_inputs():
    n = np.random.standard_normal
    s = mx_kscale(K)[:, None]
    first = np.random.permutation(np.repeat(np.arange(E), T // E))
    second = (first + 1 + np.random.permutation(np.repeat(np.arange(E - 1), -(-T // (E - 1)))[:T])) % E
    while np.bincount(second, minlength=E).max() != T // E:
        load = np.bincount(second, minlength=E); hi, lo = int(load.argmax()), int(load.argmin())
        t = np.flatnonzero((second == hi) & (first != lo))[0]; second[t] = lo
    slot_token = np.empty(E * C, np.int64); pos = np.empty((2, T), np.int64); fill = np.zeros(E, np.int64)
    place = np.stack([np.random.permutation(C) for _ in range(E)])
    for r, deal in enumerate((first, second)):
        for t in np.random.permutation(T):
            e = deal[t]; j = e * C + place[e, fill[e]]; fill[e] += 1; slot_token[j] = t; pos[r, t] = j
    g = np.random.uniform(0.2, 0.8, T)
    return {
        "xT": (n((K, T)) * s).astype(np.float32),
        "w": (n((E, K, N)) / np.sqrt(K) / s[None]).astype(np.float32),
        "b": (0.3 * n((N, E))).astype(np.float32),
        "gate": np.stack([np.tile(g, (N, 1)), np.tile(1.0 - g, (N, 1))]).astype(np.float32),
        "offs": striped(slot_token),
        "pos1": striped(pos[0]),
        "pos2": striped(pos[1]),
    }


def reference(xT, w, b, gate, offs, pos1, pos2):
    idx = unstriped(offs)
    xq = mxq(f64(xT)[:, idx], 0, "e4m3")
    y = by_expert(mxq(f64(w), 1, "e4m3"), xq)
    y = gelu(y + np.repeat(f64(b), C, axis=1))
    return f64(gate[0]) * y[:, unstriped(pos1)] + f64(gate[1]) * y[:, unstriped(pos2)]

@@ -1,0 +1,176 @@
+from contextlib import ExitStack
+
+import concourse.mybir as mybir
+
+K, T, E, C, N = 2048, 1024, 16, 128, 128
+FLOPS = 2 * K * E * C * N
+
+F32 = mybir.dt.float32
+BF16 = mybir.dt.bfloat16
+U32 = mybir.dt.uint32
+U16 = mybir.dt.uint16
+U8 = mybir.dt.uint8
+FP8X4 = mybir.dt.float8_e4m3fn_x4
+MULT, ADD = mybir.AluOpType.mult, mybir.AluOpType.add
+GELU = mybir.ActivationFunctionType.Gelu_apprx_tanh
+
+P = 128
+PASSES = K // 512
+HALF = T // 2
+SLOTS = E * C
+GROUP = 256
+EARLY = 512
+EARLY_PASSES = 2
+
+X_ON_VECTOR = (0, 1)
+W_ON_VECTOR = (7, 12)
+PIECES = (512, 256, 256)
+BYTES_PASS = PASSES
+DELAY = 2
+PER_GROUP = GROUP // C
+AHEAD = 2
+
+
+def tile_routed_moe_kernel(tc, xT, w, b, gate, offs, pos1, pos2, out):
+    nc = tc.nc
+    with ExitStack() as ctx:
+        keep = ctx.enter_context(tc.tile_pool(name="keep", bufs=1))
+        raws = ctx.enter_context(tc.tile_pool(name="raws", bufs=10))
+        stage = ctx.enter_context(tc.tile_pool(name="stage", bufs=8))
+        wts = ctx.enter_context(tc.tile_pool(name="wts", bufs=12))
+        slots_pool = ctx.enter_context(tc.tile_pool(name="slots_pool", bufs=AHEAD))
+        work = ctx.enter_context(tc.tile_pool(name="work", bufs=2))
+        psum = ctx.enter_context(tc.psum_pool(name="psum", bufs=8))
+
+        dummy = keep.tile([P, 2], F32, name="dummy")
+        nc.gpsimd.memset(dummy[:], 0.0)
+        nc.scalar.activation(dummy[:, 1:2], dummy[:, 0:1], GELU)
+        x_scales = keep.tile([P, T], U8, name="x_scales", align_bytes=64)
+        nc.gpsimd.memset(x_scales[:], 0)
+
+        offs_sb = keep.tile([P, SLOTS // 16], U16, name="offs_sb")
+        pos1_sb = keep.tile([P, T // 16], U16, name="pos1_sb")
+        pos2_sb = keep.tile([P, T // 16], U16, name="pos2_sb")
+        bias = keep.tile([P, E], F32, name="bias")
+        y = keep.tile([P, SLOTS], F32, name="y")
+        gates = keep.tile([P, 2, T], F32, name="gates")
+        x_words = []
+        for a in range(PASSES):
+            xw = keep.tile([P, T], U32, name=f"x_words{a}", align_bytes=64)
+            x_words.append(xw)
+
+        groups = {}
+        early_words = []
+        for a in range(EARLY_PASSES):
+            ew = keep.tile([P, SLOTS], U32, name=f"early_words{a}", align_bytes=64)
+            early_words.append(ew)
+
+        def gather_early(a):
+            for s in range(0, SLOTS, EARLY):
+                idx = offs_sb[:, s // 16 : (s + EARLY) // 16]
+                nc.vector.tensor_copy(early_words[a][:, s : s + EARLY], x_words[a][:].indirect(idx))
+
+        def gather_late(g):
+            idx = offs_sb[:, g * GROUP // 16 : (g + 1) * GROUP // 16]
+            for a in range(EARLY_PASSES, PASSES):
+                got = slots_pool.tile([P, GROUP], U32, name=f"slot_words{a}", align_bytes=64)
+                nc.vector.tensor_copy(got[:], x_words[a][:].indirect(idx))
+                groups[a, g] = got
+            got = slots_pool.tile([P, GROUP], U8, name="slot_scales", align_bytes=64)
+            nc.vector.tensor_copy(got[:], x_scales[:].indirect(idx))
+            groups[BYTES_PASS, g] = got
+
+        weights = {}
+
+        def multiply(e):
+            w_words, w_scales = weights[e]
+            sums = psum.tile([P, C], F32, name="sums")
+            slots = slice(e * C, (e + 1) * C)
+            g = e // PER_GROUP
+            part = slice(e % PER_GROUP * C, (e % PER_GROUP + 1) * C)
+            for a in range(PASSES):
+                words = early_words[a][:, slots] if a < EARLY_PASSES else groups[a, g][:, part]
+                nc.tensor.matmul_mx(
+                    out=sums[:],
+                    lhsT=w_words[:, a].bitcast(FP8X4),
+                    lhsT_scale=w_scales[:, a],
+                    rhs=words.bitcast(FP8X4),
+                    rhs_scale=groups[BYTES_PASS, g][4 * a : P, part],
+                    start=(a == 0),
+                    stop=(a == PASSES - 1),
+                )
+            nc.scalar.activation(y[:, slots], sums[:], GELU, bias=bias[:, e : e + 1])
+            if (e + 1) % PER_GROUP == 0 and g + AHEAD < SLOTS // GROUP:
+                gather_late(g + AHEAD)
+
+        for i in range(2 * PASSES):
+            a, h = divmod(i, 2)
+            cols = slice(h * HALF, (h + 1) * HALF)
+            raw = raws.tile([P, 4, HALF], F32, name="raw")
+            nc.sync.dma_start(
+                out=raw[:],
+                in_=xT[a * 512 : (a + 1) * 512, cols].rearrange("(p j) t -> p j t", j=4),
+            )
+            if i == 0:
+                nc.sync.dma_start(offs_sb[:], offs)
+            grouped = stage.tile([P, HALF, 4], BF16, name="grouped", align_bytes=64)
+            src = raw[:].rearrange("p j (c i) -> p c j i", i=4)
+            dst = grouped[:].rearrange("p (c i) j -> p c j i", i=4)
+            if i in X_ON_VECTOR:
+                nc.vector.tensor_copy(dst, src)
+            else:
+                nc.scalar.copy(dst, src)
+            nc.vector.quantize_mx(
+                out=x_words[a][:, cols].bitcast(FP8X4),
+                scales=x_scales[4 * a : P, cols],
+                in_=grouped[:].rearrange("p t j -> p (t j)"),
+            )
+            if h == 1 and a < EARLY_PASSES:
+                gather_early(a)
+        for g in range(AHEAD):
+            gather_late(g)
+
+        nc.sync.dma_start(bias[:], b)
+        for e in range(E):
+            cuts = ((0, 2, False), (2, 3, False), (3, 4, True)) if e == E - 1 else ((0, PASSES, e in W_ON_VECTOR),)
+            w_words = wts.tile([P, PASSES, N], U32, name="w_words", align_bytes=64)
+            w_scales = wts.tile([P, PASSES, N], U8, name="w_scales", align_bytes=64)
+            rows = w[e].rearrange("(a p j) n -> p a j n", p=P, j=4)
+            for a0, a1, on_vector in cuts:
+                raw = raws.tile([P, a1 - a0, 4, N], F32, name="raw")
+                nc.sync.dma_start(out=raw[:], in_=rows[:, a0:a1])
+                grouped = stage.tile([P, a1 - a0, N, 4], BF16, name="grouped", align_bytes=64)
+                src = raw[:].rearrange("p a j (c i) -> p a c j i", i=4)
+                dst = grouped[:].rearrange("p a (c i) j -> p a c j i", i=4)
+                if on_vector:
+                    nc.vector.tensor_copy(dst, src)
+                else:
+                    nc.scalar.copy(dst, src)
+                nc.vector.quantize_mx(
+                    out=w_words[:, a0:a1].rearrange("p a n -> p (a n)").bitcast(FP8X4),
+                    scales=w_scales[:, a0:a1].rearrange("p a n -> p (a n)"),
+                    in_=grouped[:].rearrange("p a n j -> p (a n j)"),
+                )
+            if e == 1:
+                nc.sync.dma_start(pos1_sb[:], pos1)
+                nc.sync.dma_start(pos2_sb[:], pos2)
+            weights[e] = (w_words, w_scales)
+            if e >= DELAY:
+                multiply(e - DELAY)
+        for g in range(2):
+            nc.sync.dma_start(gates[:, g], gate[g])
+        for e in range(E - DELAY, E):
+            multiply(e)
+
+        t = 0
+        for width in PIECES:
+            cols = slice(t, t + width)
+            idx = slice(t // 16, (t + width) // 16)
+            first = work.tile([P, width], F32, name="first")
+            second = work.tile([P, width], F32, name="second")
+            total = work.tile([P, width], F32, name="total")
+            nc.vector.tensor_tensor(first[:], y[:].indirect(pos1_sb[:, idx]), gates[:, 0, cols], MULT)
+            nc.vector.tensor_tensor(second[:], y[:].indirect(pos2_sb[:, idx]), gates[:, 1, cols], MULT)
+            nc.vector.tensor_tensor(total[:], first[:], second[:], ADD)
+            nc.sync.dma_start(out=out[:, cols], in_=total[:])
+            t += width

@@ -23,12 +23,14 @@ EARLY = 512
 EARLY_PASSES = 2
 
 X_ON_VECTOR = (0, 1)
-W_ON_VECTOR = (7, 12)
-PIECES = (512, 256, 256)
+W_ON_VECTOR = (4, 8, 11, 13)
+BIAS_GROUP = 4
+BIAS_LAG = 5
+PIECES = (512, 352, 160)
 BYTES_PASS = PASSES
-DELAY = 2
+DELAY = 5
 PER_GROUP = GROUP // C
-AHEAD = 2
+AHEAD = 3
 
 
 def tile_routed_moe_kernel(tc, xT, w, b, gate, offs, pos1, pos2, out):
@@ -36,7 +38,7 @@ def tile_routed_moe_kernel(tc, xT, w, b, gate, offs, pos1, pos2, out):
     with ExitStack() as ctx:
         keep = ctx.enter_context(tc.tile_pool(name="keep", bufs=1))
         raws = ctx.enter_context(tc.tile_pool(name="raws", bufs=10))
-        stage = ctx.enter_context(tc.tile_pool(name="stage", bufs=8))
+        stage = ctx.enter_context(tc.tile_pool(name="stage", bufs=10))
         wts = ctx.enter_context(tc.tile_pool(name="wts", bufs=12))
         slots_pool = ctx.enter_context(tc.tile_pool(name="slots_pool", bufs=AHEAD))
         work = ctx.enter_context(tc.tile_pool(name="work", bufs=2))
@@ -51,7 +53,6 @@ def tile_routed_moe_kernel(tc, xT, w, b, gate, offs, pos1, pos2, out):
         offs_sb = keep.tile([P, SLOTS // 16], U16, name="offs_sb")
         pos1_sb = keep.tile([P, T // 16], U16, name="pos1_sb")
         pos2_sb = keep.tile([P, T // 16], U16, name="pos2_sb")
-        bias = keep.tile([P, E], F32, name="bias")
         y = keep.tile([P, SLOTS], F32, name="y")
         gates = keep.tile([P, 2, T], F32, name="gates")
         x_words = []
@@ -81,6 +82,15 @@ def tile_routed_moe_kernel(tc, xT, w, b, gate, offs, pos1, pos2, out):
             groups[BYTES_PASS, g] = got
 
         weights = {}
+        biases = {}
+
+        def load_biases(after):
+            for e0 in range(0, E, BIAS_GROUP):
+                if min(e0 + BIAS_LAG, E - 1) == after:
+                    bias = keep.tile([P, BIAS_GROUP], F32, name=f"bias{e0}")
+                    nc.sync.dma_start(bias[:], b[:, e0 : e0 + BIAS_GROUP])
+                    for e in range(e0, e0 + BIAS_GROUP):
+                        biases[e] = bias[:, e - e0 : e - e0 + 1]
 
         def multiply(e):
             w_words, w_scales = weights[e]
@@ -99,7 +109,7 @@ def tile_routed_moe_kernel(tc, xT, w, b, gate, offs, pos1, pos2, out):
                     start=(a == 0),
                     stop=(a == PASSES - 1),
                 )
-            nc.scalar.activation(y[:, slots], sums[:], GELU, bias=bias[:, e : e + 1])
+            nc.scalar.activation(y[:, slots], sums[:], GELU, bias=biases[e])
             if (e + 1) % PER_GROUP == 0 and g + AHEAD < SLOTS // GROUP:
                 gather_late(g + AHEAD)
 
@@ -130,9 +140,8 @@ def tile_routed_moe_kernel(tc, xT, w, b, gate, offs, pos1, pos2, out):
         for g in range(AHEAD):
             gather_late(g)
 
-        nc.sync.dma_start(bias[:], b)
         for e in range(E):
-            cuts = ((0, 2, False), (2, 3, False), (3, 4, True)) if e == E - 1 else ((0, PASSES, e in W_ON_VECTOR),)
+            cuts = ((0, 2, True), (2, 4, False)) if e == E - 1 else ((0, PASSES, e in W_ON_VECTOR),)
             w_words = wts.tile([P, PASSES, N], U32, name="w_words", align_bytes=64)
             w_scales = wts.tile([P, PASSES, N], U8, name="w_scales", align_bytes=64)
             rows = w[e].rearrange("(a p j) n -> p a j n", p=P, j=4)
@@ -155,6 +164,7 @@ def tile_routed_moe_kernel(tc, xT, w, b, gate, offs, pos1, pos2, out):
                 nc.sync.dma_start(pos1_sb[:], pos1)
                 nc.sync.dma_start(pos2_sb[:], pos2)
             weights[e] = (w_words, w_scales)
+            load_biases(e)
             if e >= DELAY:
                 multiply(e - DELAY)
         for g in range(2):

@@ -18,15 +18,15 @@ P = 128
 PASSES = K // 512
 HALF = T // 2
 SLOTS = E * C
-GROUP = 256
+GROUP = 512
 EARLY = 512
 EARLY_PASSES = 2
 
 X_ON_VECTOR = (0, 1)
-W_ON_VECTOR = (4, 8, 11, 13)
+W_ON_VECTOR = (7, 10, 11, 13)
 BIAS_GROUP = 4
 BIAS_LAG = 5
-PIECES = (512, 352, 160)
+PIECES = (448, 416, 160)
 BYTES_PASS = PASSES
 DELAY = 5
 PER_GROUP = GROUP // C
@@ -38,10 +38,10 @@ def tile_routed_moe_kernel(tc, xT, w, b, gate, offs, pos1, pos2, out):
     with ExitStack() as ctx:
         keep = ctx.enter_context(tc.tile_pool(name="keep", bufs=1))
         raws = ctx.enter_context(tc.tile_pool(name="raws", bufs=10))
-        stage = ctx.enter_context(tc.tile_pool(name="stage", bufs=10))
+        stage = ctx.enter_context(tc.tile_pool(name="stage", bufs=8))
         wts = ctx.enter_context(tc.tile_pool(name="wts", bufs=12))
         slots_pool = ctx.enter_context(tc.tile_pool(name="slots_pool", bufs=AHEAD))
-        work = ctx.enter_context(tc.tile_pool(name="work", bufs=2))
+        work = ctx.enter_context(tc.tile_pool(name="work", bufs=3))
         psum = ctx.enter_context(tc.psum_pool(name="psum", bufs=8))
 
         dummy = keep.tile([P, 2], F32, name="dummy")
@@ -141,7 +141,7 @@ def tile_routed_moe_kernel(tc, xT, w, b, gate, offs, pos1, pos2, out):
             gather_late(g)
 
         for e in range(E):
-            cuts = ((0, 2, True), (2, 4, False)) if e == E - 1 else ((0, PASSES, e in W_ON_VECTOR),)
+            cuts = ((0, 2, True), (2, 3, False), (3, 4, False)) if e == E - 1 else ((0, PASSES, e in W_ON_VECTOR),)
             w_words = wts.tile([P, PASSES, N], U32, name="w_words", align_bytes=64)
             w_scales = wts.tile([P, PASSES, N], U8, name="w_scales", align_bytes=64)
             rows = w[e].rearrange("(a p j) n -> p a j n", p=P, j=4)
@@ -167,20 +167,21 @@ def tile_routed_moe_kernel(tc, xT, w, b, gate, offs, pos1, pos2, out):
             load_biases(e)
             if e >= DELAY:
                 multiply(e - DELAY)
-        for g in range(2):
-            nc.sync.dma_start(gates[:, g], gate[g])
+        nc.sync.dma_start(gates[:, 0], gate[0])
+        for cols in (slice(0, PIECES[0]), slice(PIECES[0], T)):
+            nc.sync.dma_start(gates[:, 1, cols], gate[1, :, cols])
         for e in range(E - DELAY, E):
             multiply(e)
 
+        first = keep.tile([P, T], F32, name="first")
+        nc.vector.tensor_tensor(first[:], y[:].indirect(pos1_sb[:]), gates[:, 0], MULT)
         t = 0
         for width in PIECES:
             cols = slice(t, t + width)
             idx = slice(t // 16, (t + width) // 16)
-            first = work.tile([P, width], F32, name="first")
             second = work.tile([P, width], F32, name="second")
             total = work.tile([P, width], F32, name="total")
-            nc.vector.tensor_tensor(first[:], y[:].indirect(pos1_sb[:, idx]), gates[:, 0, cols], MULT)
             nc.vector.tensor_tensor(second[:], y[:].indirect(pos2_sb[:, idx]), gates[:, 1, cols], MULT)
-            nc.vector.tensor_tensor(total[:], first[:], second[:], ADD)
+            nc.vector.tensor_tensor(total[:], first[:, cols], second[:], ADD)
             nc.sync.dma_start(out=out[:, cols], in_=total[:])
             t += width

from contextlib import ExitStack

import concourse.mybir as mybir

K, T, E, C, N = 2048, 1024, 16, 128, 128
FLOPS = 2 * K * E * C * N

F32 = mybir.dt.float32
BF16 = mybir.dt.bfloat16
U32 = mybir.dt.uint32
U16 = mybir.dt.uint16
U8 = mybir.dt.uint8
FP8X4 = mybir.dt.float8_e4m3fn_x4
MULT, ADD = mybir.AluOpType.mult, mybir.AluOpType.add
GELU = mybir.ActivationFunctionType.Gelu_apprx_tanh

P = 128
PASSES = K // 512
HALF = T // 2
SLOTS = E * C
GROUP = 512
EARLY = 512
EARLY_PASSES = 2

X_ON_VECTOR = (0, 1)
W_ON_VECTOR = (7, 10, 11, 13)
BIAS_GROUP = 4
BIAS_LAG = 5
PIECES = (448, 416, 160)
BYTES_PASS = PASSES
DELAY = 5
PER_GROUP = GROUP // C
AHEAD = 3


def tile_routed_moe_kernel(tc, xT, w, b, gate, offs, pos1, pos2, out):
    nc = tc.nc
    with ExitStack() as ctx:
        keep = ctx.enter_context(tc.tile_pool(name="keep", bufs=1))
        raws = ctx.enter_context(tc.tile_pool(name="raws", bufs=10))
        stage = ctx.enter_context(tc.tile_pool(name="stage", bufs=8))
        wts = ctx.enter_context(tc.tile_pool(name="wts", bufs=12))
        slots_pool = ctx.enter_context(tc.tile_pool(name="slots_pool", bufs=AHEAD))
        work = ctx.enter_context(tc.tile_pool(name="work", bufs=3))
        psum = ctx.enter_context(tc.psum_pool(name="psum", bufs=8))

        dummy = keep.tile([P, 2], F32, name="dummy")
        nc.gpsimd.memset(dummy[:], 0.0)
        nc.scalar.activation(dummy[:, 1:2], dummy[:, 0:1], GELU)
        x_scales = keep.tile([P, T], U8, name="x_scales", align_bytes=64)
        nc.gpsimd.memset(x_scales[:], 0)

        offs_sb = keep.tile([P, SLOTS // 16], U16, name="offs_sb")
        pos1_sb = keep.tile([P, T // 16], U16, name="pos1_sb")
        pos2_sb = keep.tile([P, T // 16], U16, name="pos2_sb")
        y = keep.tile([P, SLOTS], F32, name="y")
        gates = keep.tile([P, 2, T], F32, name="gates")
        x_words = []
        for a in range(PASSES):
            xw = keep.tile([P, T], U32, name=f"x_words{a}", align_bytes=64)
            x_words.append(xw)

        groups = {}
        early_words = []
        for a in range(EARLY_PASSES):
            ew = keep.tile([P, SLOTS], U32, name=f"early_words{a}", align_bytes=64)
            early_words.append(ew)

        def gather_early(a):
            for s in range(0, SLOTS, EARLY):
                idx = offs_sb[:, s // 16 : (s + EARLY) // 16]
                nc.vector.tensor_copy(early_words[a][:, s : s + EARLY], x_words[a][:].indirect(idx))

        def gather_late(g):
            idx = offs_sb[:, g * GROUP // 16 : (g + 1) * GROUP // 16]
            for a in range(EARLY_PASSES, PASSES):
                got = slots_pool.tile([P, GROUP], U32, name=f"slot_words{a}", align_bytes=64)
                nc.vector.tensor_copy(got[:], x_words[a][:].indirect(idx))
                groups[a, g] = got
            got = slots_pool.tile([P, GROUP], U8, name="slot_scales", align_bytes=64)
            nc.vector.tensor_copy(got[:], x_scales[:].indirect(idx))
            groups[BYTES_PASS, g] = got

        weights = {}
        biases = {}

        def load_biases(after):
            for e0 in range(0, E, BIAS_GROUP):
                if min(e0 + BIAS_LAG, E - 1) == after:
                    bias = keep.tile([P, BIAS_GROUP], F32, name=f"bias{e0}")
                    nc.sync.dma_start(bias[:], b[:, e0 : e0 + BIAS_GROUP])
                    for e in range(e0, e0 + BIAS_GROUP):
                        biases[e] = bias[:, e - e0 : e - e0 + 1]

        def multiply(e):
            w_words, w_scales = weights[e]
            sums = psum.tile([P, C], F32, name="sums")
            slots = slice(e * C, (e + 1) * C)
            g = e // PER_GROUP
            part = slice(e % PER_GROUP * C, (e % PER_GROUP + 1) * C)
            for a in range(PASSES):
                words = early_words[a][:, slots] if a < EARLY_PASSES else groups[a, g][:, part]
                nc.tensor.matmul_mx(
                    out=sums[:],
                    lhsT=w_words[:, a].bitcast(FP8X4),
                    lhsT_scale=w_scales[:, a],
                    rhs=words.bitcast(FP8X4),
                    rhs_scale=groups[BYTES_PASS, g][4 * a : P, part],
                    start=(a == 0),
                    stop=(a == PASSES - 1),
                )
            nc.scalar.activation(y[:, slots], sums[:], GELU, bias=biases[e])
            if (e + 1) % PER_GROUP == 0 and g + AHEAD < SLOTS // GROUP:
                gather_late(g + AHEAD)

        for i in range(2 * PASSES):
            a, h = divmod(i, 2)
            cols = slice(h * HALF, (h + 1) * HALF)
            raw = raws.tile([P, 4, HALF], F32, name="raw")
            nc.sync.dma_start(
                out=raw[:],
                in_=xT[a * 512 : (a + 1) * 512, cols].rearrange("(p j) t -> p j t", j=4),
            )
            if i == 0:
                nc.sync.dma_start(offs_sb[:], offs)
            grouped = stage.tile([P, HALF, 4], BF16, name="grouped", align_bytes=64)
            src = raw[:].rearrange("p j (c i) -> p c j i", i=4)
            dst = grouped[:].rearrange("p (c i) j -> p c j i", i=4)
            if i in X_ON_VECTOR:
                nc.vector.tensor_copy(dst, src)
            else:
                nc.scalar.copy(dst, src)
            nc.vector.quantize_mx(
                out=x_words[a][:, cols].bitcast(FP8X4),
                scales=x_scales[4 * a : P, cols],
                in_=grouped[:].rearrange("p t j -> p (t j)"),
            )
            if h == 1 and a < EARLY_PASSES:
                gather_early(a)
        for g in range(AHEAD):
            gather_late(g)

        for e in range(E):
            cuts = ((0, 2, True), (2, 3, False), (3, 4, False)) if e == E - 1 else ((0, PASSES, e in W_ON_VECTOR),)
            w_words = wts.tile([P, PASSES, N], U32, name="w_words", align_bytes=64)
            w_scales = wts.tile([P, PASSES, N], U8, name="w_scales", align_bytes=64)
            rows = w[e].rearrange("(a p j) n -> p a j n", p=P, j=4)
            for a0, a1, on_vector in cuts:
                raw = raws.tile([P, a1 - a0, 4, N], F32, name="raw")
                nc.sync.dma_start(out=raw[:], in_=rows[:, a0:a1])
                grouped = stage.tile([P, a1 - a0, N, 4], BF16, name="grouped", align_bytes=64)
                src = raw[:].rearrange("p a j (c i) -> p a c j i", i=4)
                dst = grouped[:].rearrange("p a (c i) j -> p a c j i", i=4)
                if on_vector:
                    nc.vector.tensor_copy(dst, src)
                else:
                    nc.scalar.copy(dst, src)
                nc.vector.quantize_mx(
                    out=w_words[:, a0:a1].rearrange("p a n -> p (a n)").bitcast(FP8X4),
                    scales=w_scales[:, a0:a1].rearrange("p a n -> p (a n)"),
                    in_=grouped[:].rearrange("p a n j -> p (a n j)"),
                )
            if e == 1:
                nc.sync.dma_start(pos1_sb[:], pos1)
                nc.sync.dma_start(pos2_sb[:], pos2)
            weights[e] = (w_words, w_scales)
            load_biases(e)
            if e >= DELAY:
                multiply(e - DELAY)
        nc.sync.dma_start(gates[:, 0], gate[0])
        for cols in (slice(0, PIECES[0]), slice(PIECES[0], T)):
            nc.sync.dma_start(gates[:, 1, cols], gate[1, :, cols])
        for e in range(E - DELAY, E):
            multiply(e)

        first = keep.tile([P, T], F32, name="first")
        nc.vector.tensor_tensor(first[:], y[:].indirect(pos1_sb[:]), gates[:, 0], MULT)
        t = 0
        for width in PIECES:
            cols = slice(t, t + width)
            idx = slice(t // 16, (t + width) // 16)
            second = work.tile([P, width], F32, name="second")
            total = work.tile([P, width], F32, name="total")
            nc.vector.tensor_tensor(second[:], y[:].indirect(pos2_sb[:, idx]), gates[:, 1, cols], MULT)
            nc.vector.tensor_tensor(total[:], first[:, cols], second[:], ADD)
            nc.sync.dma_start(out=out[:, cols], in_=total[:])
            t += width
